import numpy as np
import ml_dtypes


def mxq(x, axis, fmt="e4m3"):
    dtype, down = {"e4m3": (ml_dtypes.float8_e4m3fn, 7), "e5m2": (ml_dtypes.float8_e5m2, 14)}[fmt]
    v = np.moveaxis(np.asarray(x, np.float32).astype(ml_dtypes.bfloat16).astype(np.float64), axis, -1)
    blocks = v.reshape(v.shape[:-1] + (-1, 32))
    amax = np.abs(blocks).max(-1, keepdims=True)
    byte = np.maximum(np.where(amax > 0, np.frexp(amax)[1] - 1 + 127, 0) - down, 1)
    scale = np.exp2(byte - 127.0)
    codes = (blocks / scale).astype(np.float32).astype(dtype).astype(np.float64)
    return np.moveaxis((codes * scale).reshape(v.shape), -1, axis)


WIDE = False


def mx_kscale(k):
    if not WIDE:
        return np.ones(k)
    levels = np.array([10, -10, 5, -5, 0])
    if k % 512:
        return np.exp2(np.random.permutation(np.resize(levels, k // 32))).repeat(32)
    a = np.empty((k // 512, 16))
    for p in range(k // 512):
        a[p, :8] = np.random.permutation(np.resize(levels, 8))
        for g in range(8):
            far = levels[np.abs(levels - a[p, g]) >= 10]
            a[p, g + 8] = far[np.random.randint(len(far))]
    return np.exp2(a.ravel()).repeat(32)


def f64(x):
    return np.asarray(x).astype(np.float64)


def striped(idx):
    return np.tile(idx.reshape(-1, 16).T, (8, 1)).astype(np.uint16)


def unstriped(offs):
    return offs[:16].T.reshape(-1).astype(np.int64)


def pack_weight(w):
    k, n = w.shape
    w = f64(np.asarray(w, np.float32).astype(ml_dtypes.bfloat16)).reshape(k // 32, 32, n)
    amax = np.abs(w).max(1)
    byte = np.clip(np.where(amax > 0, np.frexp(amax)[1] - 1 + 127 - 7, 1), 1, 254)
    scaled = (w * np.exp2(127.0 - byte)[:, None, :]).reshape(k, n).astype(np.float32)
    words = np.ascontiguousarray(scaled.reshape(k // 512, 128, 4, n).transpose(0, 1, 3, 2)).astype(ml_dtypes.float8_e4m3fn).view(np.uint8)
    return words, np.ascontiguousarray(byte.astype(np.uint8).reshape(k // 512, 16, n))


def unpack_weight(words, scales):
    g, p, n, _ = words.shape
    vals = np.ascontiguousarray(words).view(ml_dtypes.float8_e4m3fn).astype(np.float64) * np.repeat(np.exp2(scales.astype(np.float64) - 127.0), 8, axis=1)[..., None]
    return vals.transpose(0, 1, 3, 2).reshape(g * 512, n)


E2M1 = np.array([0.0, 0.5, 1.0, 1.5, 2.0, 3.0, 4.0, 6.0, -0.0, -0.5, -1.0, -1.5, -2.0, -3.0, -4.0, -6.0])


def pack_fp4(w):
    k, n = w.shape
    w = f64(np.asarray(w, np.float32).astype(ml_dtypes.bfloat16)).reshape(k // 32, 32, n)
    amax = np.abs(w).max(1)
    mant, ex = np.frexp(amax / 6.0)
    byte = np.clip(np.where(amax > 0, np.where(mant > 0.5, ex, ex - 1) + 127, 1), 1, 254)
    scaled = (w * np.exp2(127.0 - byte)[:, None, :]).reshape(k, n).astype(np.float32)
    c = np.ascontiguousarray(scaled.reshape(k // 512, 128, 4, n).transpose(0, 1, 3, 2)).astype(ml_dtypes.float4_e2m1fn).view(np.uint8) & 0xF
    words = (c[..., 0::2] | (c[..., 1::2] << 4)).reshape(k // 512, 128, 2 * n)
    return np.ascontiguousarray(words), np.ascontiguousarray(byte.astype(np.uint8).reshape(k // 512, 16, n))


def unpack_fp4(words, scales):
    g, _, n = scales.shape
    words = np.ascontiguousarray(words).reshape(g, 128, n, 2)
    nib = np.empty((g, 128, n, 4), np.uint8)
    nib[..., 0::2] = words & 0xF
    nib[..., 1::2] = words >> 4
    vals = E2M1[nib] * np.repeat(np.exp2(scales.astype(np.float64) - 127.0), 8, axis=1)[..., None]
    return vals.transpose(0, 1, 3, 2).reshape(g * 512, n)


K, T, D, H, N = 512, 1024, 2, 512, 128
P = 2 ** 7


def setup_inputs():
    n = np.random.standard_normal
    s = mx_kscale(K)[:, None]
    u = mx_kscale(H)
    packed_xT = pack_weight(n((K, T)) * s)
    packed_w2 = pack_fp4(n((H, N)) / np.sqrt(H) / u[:, None])
    return {
        "x_words": packed_xT[0],
        "x_scales": packed_xT[1],
        "w1": (n((K, H)) / np.sqrt(K) / s * u).astype(np.float32),
        "w2_words": packed_w2[0],
        "w2_scales": packed_w2[1],
        "gate": (np.tile(np.random.uniform(0.2, 1.0, (D, 1, T)) / np.sqrt(D), (1, P, 1))).astype(np.float32),
        "pos1": striped(np.random.permutation(T)),
        "pos2": striped(np.random.permutation(T)),
    }


def reference(x_words, x_scales, w1, w2_words, w2_scales, gate, pos1, pos2):
    xq = unpack_weight(x_words, x_scales)
    h = mxq(f64(w1), 0, "e4m3").T @ xq
    z = h - (h[:, unstriped(pos1)] * f64(gate)[0, :1] + h[:, unstriped(pos2)] * f64(gate)[1, :1])
    return unpack_fp4(w2_words, w2_scales).T @ mxq(z, 0, "e4m3")

@@ -1,0 +1,220 @@
+from contextlib import ExitStack
+
+import concourse.mybir as mybir
+from concourse.masks import make_identity
+
+K, T, H, N = 512, 1024, 512, 128
+FLOPS = 2 * K * H * T + 2 * H * N * T
+
+F32 = mybir.dt.float32
+BF16 = mybir.dt.bfloat16
+I32 = mybir.dt.int32
+U32 = mybir.dt.uint32
+U16 = mybir.dt.uint16
+U8 = mybir.dt.uint8
+FP8X4 = mybir.dt.float8_e4m3fn_x4
+FP4X4 = mybir.dt.float4_e2m1fn_x4
+MULT = mybir.AluOpType.mult
+
+P = 128
+PACK = 4
+BANK = 512
+TILES = H // P
+CHUNKS = ((0, 512), (512, 384), (896, 128))
+PIECES = {512: (512,), 384: (256, 128), 256: (256,), 128: (128,)}
+
+
+def tile_picked_wlapl_none_l_kernel(
+    tc, x_words, x_scales, w1, w2_words, w2_scales, gate, pos1, pos2, out
+):
+    nc = tc.nc
+    with ExitStack() as ctx:
+        lists = ctx.enter_context(tc.tile_pool(name="lists", bufs=1))
+        keep = ctx.enter_context(tc.tile_pool(name="keep", bufs=1))
+        ring = ctx.enter_context(tc.tile_pool(name="ring", bufs=4))
+        psum = ctx.enter_context(tc.psum_pool(name="psum", bufs=1))
+
+        def bank(index, name):
+            return psum.tile([P, BANK], F32, name=name, tag="bank%d" % (index % 8))
+
+        ident = keep.tile([P, P], F32, name="ident")
+        make_identity(nc, ident[:])
+
+        x_plane = keep.tile([P, T], U8, name="x_plane", align_bytes=64)
+        w2_plane = keep.tile([P, N], U8, name="w2_plane", align_bytes=64)
+        nc.vector.memset(x_plane[:].bitcast(I32), 0)
+        nc.vector.memset(w2_plane[:].bitcast(I32), 0)
+
+        w1_rows = w1.rearrange("(p j) c -> p j c", j=PACK)
+        w1_raw = [keep.tile([P, PACK, P], F32, name="w1_raw%d" % t) for t in range(TILES)]
+        x_codes = keep.tile([P, T], U32, name="x_codes", align_bytes=64)
+        gate_cols = [keep.tile([P, 2, PACK], F32, name="gate_cols%d" % d) for d in range(2)]
+        offsets = [lists.tile([P, T // 16], U16, name="offsets%d" % d) for d in range(2)]
+        w2_codes = keep.tile([P, 2 * N], U8, name="w2_codes", align_bytes=64)
+
+        def load_gate(d):
+            nc.sync.dma_start(out=gate_cols[d][:], in_=gate[d, 0, :].rearrange("(b p j) -> p b j", b=2, j=PACK))
+
+        nc.sync.dma_start(out=w1_raw[0][:], in_=w1_rows[:, :, 0:P])
+        for q in range(4):
+            nc.scalar.dma_start(
+                out=x_plane[32 * q : 32 * q + 4, :].bitcast(I32),
+                in_=x_scales[0, 4 * q : 4 * q + 4, :].bitcast(I32),
+            )
+        load_gate(0)
+        nc.sync.dma_start(
+            out=x_codes[:].bitcast(I32), in_=x_words[0].rearrange("p c r -> p (c r)").bitcast(I32)
+        )
+        load_gate(1)
+        nc.sync.dma_start(offsets[0][:], pos1)
+        nc.sync.dma_start(out=w1_raw[1][:], in_=w1_rows[:, :, P : 2 * P])
+        nc.sync.dma_start(offsets[1][:], pos2)
+        for t in range(2, TILES):
+            nc.sync.dma_start(out=w1_raw[t][:], in_=w1_rows[:, :, t * P : (t + 1) * P])
+        nc.sync.dma_start(out=w2_codes[:].bitcast(I32), in_=w2_words[0].bitcast(I32))
+        for q in range(4):
+            nc.sync.dma_start(
+                out=w2_plane[32 * q : 32 * q + 4, :].bitcast(I32),
+                in_=w2_scales[0, 4 * q : 4 * q + 4, :].bitcast(I32),
+            )
+
+        neg_cols = [keep.tile([P, 2, PACK], F32, name="neg_cols%d" % d) for d in range(2)]
+        neg_gate = [keep.tile([P, T], F32, name="neg_gate%d" % d) for d in range(2)]
+
+        def spread_gate(d, b, index):
+            spread = bank(index, "spread")
+            for j in range(PACK):
+                nc.tensor.transpose(
+                    spread[:, j * P : (j + 1) * P], neg_cols[d][:, b, j : j + 1].to_broadcast([P, P]), ident[:]
+                )
+            nc.scalar.copy(
+                out=neg_gate[d][:, b * BANK : (b + 1) * BANK].rearrange("p (i j) -> p i j", j=PACK),
+                in_=spread[:].rearrange("p (j i) -> p i j", j=PACK),
+            )
+
+        w1_codes = [keep.tile([P, P], U32, name="w1_codes%d" % t, align_bytes=64) for t in range(TILES)]
+        w1_plane = [keep.tile([P, P], U8, name="w1_plane%d" % t, align_bytes=64) for t in range(TILES)]
+        h = [keep.tile([P, T], F32, name="h%d" % t) for t in range(TILES)]
+
+        def quantize_w1(t):
+            grouped = keep.tile([P, P, PACK], BF16, name="w1_grouped%d" % t, align_bytes=64)
+            dst = grouped[:].rearrange("p (c i) j -> p c j i", i=4)
+            src = w1_raw[t][:].rearrange("p j (c i) -> p c j i", i=4)
+            if t == 0:
+                nc.vector.tensor_copy(out=dst, in_=src)
+            else:
+                nc.scalar.copy(out=dst, in_=src)
+            nc.vector.quantize_mx(
+                out=w1_codes[t][:].bitcast(FP8X4),
+                scales=w1_plane[t][:],
+                in_=grouped[:].rearrange("p c j -> p (c j)"),
+            )
+
+        def project(t):
+            for half in range(2):
+                cols = slice(half * BANK, (half + 1) * BANK)
+                acc = bank(2 + 2 * t + half, "h_acc")
+                nc.tensor.matmul_mx(
+                    out=acc[:],
+                    lhsT=w1_codes[t][:].bitcast(FP8X4),
+                    lhsT_scale=w1_plane[t][:],
+                    rhs=x_codes[:, cols].bitcast(FP8X4),
+                    rhs_scale=x_plane[:, cols],
+                    start=True,
+                    stop=True,
+                )
+                if t == 0 and half == 0:
+                    nc.vector.tensor_copy(out=h[t][:, cols], in_=acc[:])
+                else:
+                    nc.scalar.copy(out=h[t][:, cols], in_=acc[:])
+
+        for d in range(2):
+            nc.vector.tensor_scalar(neg_cols[d][:], gate_cols[d][:], -1.0, None, MULT)
+        quantize_w1(0)
+        spread_gate(0, 0, 0)
+        project(0)
+        spread_gate(1, 0, 1)
+        quantize_w1(1)
+        project(1)
+
+        sum_banks = (5, 7, 1, 4)
+        word_banks = (2, 3)
+        out_banks = (6, 0)
+        piece_count = 0
+        for chunk, (v0, width) in enumerate(CHUNKS):
+            blocks = width // P
+            z_rows = keep.tile([P, blocks, 2, P, 2], BF16, name="z_rows%d" % chunk)
+            for t in range(TILES):
+                if chunk == 0 and t + 2 < TILES:
+                    quantize_w1(t + 2)
+                    project(t + 2)
+                if chunk == 0 and t == 2:
+                    spread_gate(0, 1, 2)
+                    spread_gate(1, 1, 3)
+                terms = [h[t][:, v0 : v0 + width]]
+                for d in range(2):
+                    pulled = ring.tile([P, width], F32, name="pulled", tag="pulled")
+                    nc.vector.tensor_tensor(
+                        pulled[:],
+                        h[t][:].indirect(offsets[d][:, v0 // 16 : (v0 + width) // 16]),
+                        neg_gate[d][:, v0 : v0 + width],
+                        MULT,
+                    )
+                    terms.append(pulled[:])
+                sums = bank(sum_banks[t], "sums")
+                for b in range(blocks):
+                    for n, term in enumerate(terms):
+                        nc.tensor.matmul(
+                            sums[:, b * P : (b + 1) * P],
+                            term[:, b * P : (b + 1) * P],
+                            ident[:],
+                            start=(n == 0),
+                            stop=(n == len(terms) - 1),
+                            is_transpose=True,
+                        )
+                nc.scalar.copy(
+                    out=z_rows[:, :, :, 32 * t : 32 * (t + 1), :],
+                    in_=sums[:, 0:width].rearrange("v (b q u e) -> v b u q e", b=blocks, u=2, e=2),
+                )
+
+            z_words = z_rows[:].rearrange("v b u p e -> v (b u p e)").bitcast(F32)
+            z_grouped = keep.tile([P, width * PACK], BF16, name="z_grouped%d" % chunk, align_bytes=64)
+            for b0 in range(0, blocks, 2):
+                count = min(2, blocks - b0)
+                words = bank(word_banks[(b0 // 2) % 2], "words")
+                for s in range(2 * count):
+                    nc.tensor.transpose(
+                        words[:, s * P : (s + 1) * P],
+                        z_words[:, (2 * b0 + s) * P : (2 * b0 + s + 1) * P],
+                        ident[:],
+                    )
+                nc.scalar.copy(
+                    out=z_grouped[:, b0 * P * PACK : (b0 + count) * P * PACK]
+                    .bitcast(F32)
+                    .rearrange("p (b v u) -> p b v u", b=count, u=2),
+                    in_=words[:, 0 : 2 * count * P].rearrange("p (b u v) -> p b v u", b=count, u=2),
+                )
+            c0 = 0
+            for piece in PIECES[width]:
+                z_codes = keep.tile([P, piece], U32, name="z_codes%d" % piece_count, align_bytes=64)
+                z_plane = keep.tile([P, piece], U8, name="z_plane%d" % piece_count, align_bytes=64)
+                nc.vector.quantize_mx(
+                    out=z_codes[:].bitcast(FP8X4),
+                    scales=z_plane[:],
+                    in_=z_grouped[:, c0 * PACK : (c0 + piece) * PACK],
+                )
+                acc = bank(out_banks[piece_count % 2], "out_acc")
+                nc.tensor.matmul_mx(
+                    out=acc[:, 0:piece],
+                    lhsT=w2_codes[:].bitcast(FP4X4),
+                    lhsT_scale=w2_plane[:],
+                    rhs=z_codes[:].bitcast(FP8X4),
+                    rhs_scale=z_plane[:],
+                    start=True,
+                    stop=True,
+                )
+                result = keep.tile([P, piece], F32, name="result%d" % piece_count)
+                nc.scalar.copy(out=result[:], in_=acc[:, 0:piece])
+                nc.sync.dma_start(out=out[:, v0 + c0 : v0 + c0 + piece], in_=result[:])
+                c0 += piece
+                piece_count += 1

@@ -15,12 +15,15 @@ U8 = mybir.dt.uint8
 FP8X4 = mybir.dt.float8_e4m3fn_x4
 FP4X4 = mybir.dt.float4_e2m1fn_x4
 MULT = mybir.AluOpType.mult
+COPY = mybir.ActivationFunctionType.Copy
 
 P = 128
 PACK = 4
 BANK = 512
 TILES = H // P
 CHUNKS = ((0, 512), (512, 384), (896, 128))
+SLOTS = 6
+AHEAD = 1
 PIECES = {512: (512,), 384: (256, 128), 256: (256,), 128: (128,)}
 
 
@@ -31,76 +34,74 @@ def tile_picked_wlapl_none_l_kernel(
     with ExitStack() as ctx:
         lists = ctx.enter_context(tc.tile_pool(name="lists", bufs=1))
         keep = ctx.enter_context(tc.tile_pool(name="keep", bufs=1))
-        ring = ctx.enter_context(tc.tile_pool(name="ring", bufs=4))
+        ring = ctx.enter_context(tc.tile_pool(name="ring", bufs=1))
         psum = ctx.enter_context(tc.psum_pool(name="psum", bufs=1))
 
         def bank(index, name):
-            return psum.tile([P, BANK], F32, name=name, tag="bank%d" % (index % 8))
-
-        ident = keep.tile([P, P], F32, name="ident")
-        make_identity(nc, ident[:])
+            return psum.tile([P, BANK], F32, name=name, tag="bank%d" % index)
 
         x_plane = keep.tile([P, T], U8, name="x_plane", align_bytes=64)
         w2_plane = keep.tile([P, N], U8, name="w2_plane", align_bytes=64)
-        nc.vector.memset(x_plane[:].bitcast(I32), 0)
-        nc.vector.memset(w2_plane[:].bitcast(I32), 0)
+        ident = keep.tile([P, P], F32, name="ident")
+        make_identity(nc, ident[:])
 
         w1_rows = w1.rearrange("(p j) c -> p j c", j=PACK)
-        w1_raw = [keep.tile([P, PACK, P], F32, name="w1_raw%d" % t) for t in range(TILES)]
+        w1_loads = ((0, 1), (1, 3))
+        w1_raw = [keep.tile([P, PACK, n * P], F32, name="w1_raw%d" % t) for t, n in w1_loads]
         x_codes = keep.tile([P, T], U32, name="x_codes", align_bytes=64)
-        gate_cols = [keep.tile([P, 2, PACK], F32, name="gate_cols%d" % d) for d in range(2)]
+        gate_cols = keep.tile([P, 2, T // P], F32, name="gate_cols")
         offsets = [lists.tile([P, T // 16], U16, name="offsets%d" % d) for d in range(2)]
         w2_codes = keep.tile([P, 2 * N], U8, name="w2_codes", align_bytes=64)
 
-        def load_gate(d):
-            nc.sync.dma_start(out=gate_cols[d][:], in_=gate[d, 0, :].rearrange("(b p j) -> p b j", b=2, j=PACK))
-
+        nc.sync.dma_start(out=gate_cols[:], in_=gate[:, 0, :].rearrange("d (p j) -> p d j", p=P))
         nc.sync.dma_start(out=w1_raw[0][:], in_=w1_rows[:, :, 0:P])
         for q in range(4):
             nc.scalar.dma_start(
-                out=x_plane[32 * q : 32 * q + 4, :].bitcast(I32),
-                in_=x_scales[0, 4 * q : 4 * q + 4, :].bitcast(I32),
+                out=x_plane[32 * q : 32 * (q + 1), :].bitcast(I32),
+                in_=x_scales[0, 4 * q : 4 * q + 4, :].bitcast(I32).partition_broadcast(8),
             )
-        load_gate(0)
-        nc.sync.dma_start(
-            out=x_codes[:].bitcast(I32), in_=x_words[0].rearrange("p c r -> p (c r)").bitcast(I32)
-        )
-        load_gate(1)
+        nc.sync.dma_start(out=x_codes[:].bitcast(I32), in_=x_words[0].rearrange("p c r -> p (c r)").bitcast(I32))
         nc.sync.dma_start(offsets[0][:], pos1)
-        nc.sync.dma_start(out=w1_raw[1][:], in_=w1_rows[:, :, P : 2 * P])
+        nc.sync.dma_start(out=w1_raw[1][:], in_=w1_rows[:, :, P : 4 * P])
         nc.sync.dma_start(offsets[1][:], pos2)
-        for t in range(2, TILES):
-            nc.sync.dma_start(out=w1_raw[t][:], in_=w1_rows[:, :, t * P : (t + 1) * P])
         nc.sync.dma_start(out=w2_codes[:].bitcast(I32), in_=w2_words[0].bitcast(I32))
         for q in range(4):
             nc.sync.dma_start(
-                out=w2_plane[32 * q : 32 * q + 4, :].bitcast(I32),
-                in_=w2_scales[0, 4 * q : 4 * q + 4, :].bitcast(I32),
+                out=w2_plane[32 * q : 32 * (q + 1), :].bitcast(I32),
+                in_=w2_scales[0, 4 * q : 4 * q + 4, :].bitcast(I32).partition_broadcast(8),
             )
 
-        neg_cols = [keep.tile([P, 2, PACK], F32, name="neg_cols%d" % d) for d in range(2)]
         neg_gate = [keep.tile([P, T], F32, name="neg_gate%d" % d) for d in range(2)]
+
+        def slot_of(n):
+            return "slot%d" % (n % 4 if n < 6 else (n - 2) % SLOTS)
 
         def spread_gate(d, b, index):
             spread = bank(index, "spread")
             for j in range(PACK):
                 nc.tensor.transpose(
-                    spread[:, j * P : (j + 1) * P], neg_cols[d][:, b, j : j + 1].to_broadcast([P, P]), ident[:]
+                    spread[:, j * P : (j + 1) * P], gate_cols[:, d, PACK * b + j : PACK * b + j + 1].to_broadcast([P, P]), ident[:]
                 )
-            nc.scalar.copy(
-                out=neg_gate[d][:, b * BANK : (b + 1) * BANK].rearrange("p (i j) -> p i j", j=PACK),
+            nc.scalar.activation(
+                out=neg_gate[d][:].rearrange("p (i b j) -> p b i j", b=2, j=PACK)[:, b],
                 in_=spread[:].rearrange("p (j i) -> p i j", j=PACK),
+                func=COPY,
+                scale=-1.0,
             )
 
-        w1_codes = [keep.tile([P, P], U32, name="w1_codes%d" % t, align_bytes=64) for t in range(TILES)]
+        grouped_tags = ("slot0", "w1_codes0", "slot0", "slot1")
+        w1_codes = [
+            ring.tile([P, P], U32, name="w1_codes", tag="w1_codes%d" % t, align_bytes=64) for t in range(TILES)
+        ]
         w1_plane = [keep.tile([P, P], U8, name="w1_plane%d" % t, align_bytes=64) for t in range(TILES)]
         h = [keep.tile([P, T], F32, name="h%d" % t) for t in range(TILES)]
 
         def quantize_w1(t):
-            grouped = keep.tile([P, P, PACK], BF16, name="w1_grouped%d" % t, align_bytes=64)
+            grouped = ring.tile([P, P, PACK], BF16, name="w1_grouped", tag=grouped_tags[t], align_bytes=64)
             dst = grouped[:].rearrange("p (c i) j -> p c j i", i=4)
-            src = w1_raw[t][:].rearrange("p j (c i) -> p c j i", i=4)
-            if t == 0:
+            first = t - min(t, 1)
+            src = w1_raw[min(t, 1)][:, :, first * P : (first + 1) * P].rearrange("p j (c i) -> p c j i", i=4)
+            if t < 1:
                 nc.vector.tensor_copy(out=dst, in_=src)
             else:
                 nc.scalar.copy(out=dst, in_=src)
@@ -110,10 +111,12 @@ def tile_picked_wlapl_none_l_kernel(
                 in_=grouped[:].rearrange("p c j -> p (c j)"),
             )
 
+        h_banks = (0, 2, 0, 2)
+
         def project(t):
             for half in range(2):
                 cols = slice(half * BANK, (half + 1) * BANK)
-                acc = bank(2 + 2 * t + half, "h_acc")
+                acc = bank(h_banks[t] + half, "h_acc")
                 nc.tensor.matmul_mx(
                     out=acc[:],
                     lhsT=w1_codes[t][:].bitcast(FP8X4),
@@ -123,65 +126,42 @@ def tile_picked_wlapl_none_l_kernel(
                     start=True,
                     stop=True,
                 )
-                if t == 0 and half == 0:
+                if t == 0:
                     nc.vector.tensor_copy(out=h[t][:, cols], in_=acc[:])
                 else:
                     nc.scalar.copy(out=h[t][:, cols], in_=acc[:])
 
-        for d in range(2):
-            nc.vector.tensor_scalar(neg_cols[d][:], gate_cols[d][:], -1.0, None, MULT)
-        quantize_w1(0)
-        spread_gate(0, 0, 0)
-        project(0)
-        spread_gate(1, 0, 1)
-        quantize_w1(1)
-        project(1)
-
-        sum_banks = (5, 7, 1, 4)
-        word_banks = (2, 3)
-        out_banks = (6, 0)
-        piece_count = 0
-        for chunk, (v0, width) in enumerate(CHUNKS):
+        def turn_into(sums, term, width, first, last):
             blocks = width // P
-            z_rows = keep.tile([P, blocks, 2, P, 2], BF16, name="z_rows%d" % chunk)
-            for t in range(TILES):
-                if chunk == 0 and t + 2 < TILES:
-                    quantize_w1(t + 2)
-                    project(t + 2)
-                if chunk == 0 and t == 2:
-                    spread_gate(0, 1, 2)
-                    spread_gate(1, 1, 3)
-                terms = [h[t][:, v0 : v0 + width]]
-                for d in range(2):
-                    pulled = ring.tile([P, width], F32, name="pulled", tag="pulled")
-                    nc.vector.tensor_tensor(
-                        pulled[:],
-                        h[t][:].indirect(offsets[d][:, v0 // 16 : (v0 + width) // 16]),
-                        neg_gate[d][:, v0 : v0 + width],
-                        MULT,
-                    )
-                    terms.append(pulled[:])
-                sums = bank(sum_banks[t], "sums")
-                for b in range(blocks):
-                    for n, term in enumerate(terms):
-                        nc.tensor.matmul(
-                            sums[:, b * P : (b + 1) * P],
-                            term[:, b * P : (b + 1) * P],
-                            ident[:],
-                            start=(n == 0),
-                            stop=(n == len(terms) - 1),
-                            is_transpose=True,
-                        )
-                nc.scalar.copy(
-                    out=z_rows[:, :, :, 32 * t : 32 * (t + 1), :],
-                    in_=sums[:, 0:width].rearrange("v (b q u e) -> v b u q e", b=blocks, u=2, e=2),
+            for b in range(blocks):
+                nc.tensor.matmul(
+                    sums[:, b * P : (b + 1) * P],
+                    term[:, b * P : (b + 1) * P],
+                    ident[:],
+                    start=(first and b == 0),
+                    stop=(last and b == blocks - 1),
+                    is_transpose=True,
                 )
 
+        steps = [(0, 0), (1, 0)] + [
+            (chunk, t) for chunk in range(len(CHUNKS)) for t in range(TILES) if t > 0 or chunk > 1
+        ]
+        open_sums = {}
+
+        def open_step(s):
+            chunk, t = steps[s]
+            v0, width = CHUNKS[chunk]
+            open_sums[s] = bank(4 + s % 4, "sums")
+            turn_into(open_sums[s], h[t][:, v0 : v0 + width], width, True, False)
+
+        def finish_chunk(chunk, z_rows):
+            v0, width = CHUNKS[chunk]
+            blocks = width // P
             z_words = z_rows[:].rearrange("v b u p e -> v (b u p e)").bitcast(F32)
             z_grouped = keep.tile([P, width * PACK], BF16, name="z_grouped%d" % chunk, align_bytes=64)
             for b0 in range(0, blocks, 2):
                 count = min(2, blocks - b0)
-                words = bank(word_banks[(b0 // 2) % 2], "words")
+                words = bank((b0 // 2 + chunk) % 2, "words")
                 for s in range(2 * count):
                     nc.tensor.transpose(
                         words[:, s * P : (s + 1) * P],
@@ -194,16 +174,21 @@ def tile_picked_wlapl_none_l_kernel(
                     .rearrange("p (b v u) -> p b v u", b=count, u=2),
                     in_=words[:, 0 : 2 * count * P].rearrange("p (b u v) -> p b v u", b=count, u=2),
                 )
+            return z_grouped
+
+        def project_chunk(chunk, z_grouped):
+            v0, width = CHUNKS[chunk]
             c0 = 0
-            for piece in PIECES[width]:
-                z_codes = keep.tile([P, piece], U32, name="z_codes%d" % piece_count, align_bytes=64)
-                z_plane = keep.tile([P, piece], U8, name="z_plane%d" % piece_count, align_bytes=64)
+            for n, piece in enumerate(PIECES[width]):
+                tag = slot_of(len(pulls) - 2) if chunk == 0 else "z_codes%d_%d" % (chunk, n)
+                z_codes = ring.tile([P, piece], U32, name="z_codes", tag=tag, align_bytes=64)
+                z_plane = keep.tile([P, piece], U8, name="z_plane%d_%d" % (chunk, n), align_bytes=64)
                 nc.vector.quantize_mx(
                     out=z_codes[:].bitcast(FP8X4),
                     scales=z_plane[:],
                     in_=z_grouped[:, c0 * PACK : (c0 + piece) * PACK],
                 )
-                acc = bank(out_banks[piece_count % 2], "out_acc")
+                acc = bank((2, 4, 3)[chunk] + n, "out_acc")
                 nc.tensor.matmul_mx(
                     out=acc[:, 0:piece],
                     lhsT=w2_codes[:].bitcast(FP4X4),
@@ -213,8 +198,53 @@ def tile_picked_wlapl_none_l_kernel(
                     start=True,
                     stop=True,
                 )
-                result = keep.tile([P, piece], F32, name="result%d" % piece_count)
-                nc.scalar.copy(out=result[:], in_=acc[:, 0:piece])
+                result = keep.tile([P, piece], F32, name="result%d_%d" % (chunk, n))
+                if chunk == 0:
+                    nc.vector.tensor_copy(out=result[:], in_=acc[:, 0:piece])
+                else:
+                    nc.scalar.copy(out=result[:], in_=acc[:, 0:piece])
                 nc.sync.dma_start(out=out[:, v0 + c0 : v0 + c0 + piece], in_=result[:])
                 c0 += piece
-                piece_count += 1
+
+        spread_gate(0, 0, 0)
+        spread_gate(0, 1, 1)
+        quantize_w1(0)
+        project(0)
+        spread_gate(1, 0, 0)
+        spread_gate(1, 1, 1)
+        quantize_w1(1)
+        project(1)
+
+        z_rows = [
+            keep.tile([P, width // P, 2, P, 2], BF16, name="z_rows%d" % chunk)
+            for chunk, (v0, width) in enumerate(CHUNKS)
+        ]
+        grouped_z = []
+        pulls = [(0, 0), (1, 0), (0, 1), (1, 1)] + [(s, d) for s in range(2, len(steps)) for d in range(2)]
+        for n, (s, d) in enumerate(pulls):
+            chunk, t = steps[s]
+            v0, width = CHUNKS[chunk]
+            if n in (1, 2):
+                quantize_w1(n + 1)
+                project(n + 1)
+            for ahead in range(s, min(s + AHEAD + 1, len(steps))):
+                if ahead not in open_sums:
+                    open_step(ahead)
+            sums = open_sums[s]
+            pulled = ring.tile([P, width], F32, name="pulled", tag=slot_of(n), align_bytes=64)
+            nc.vector.tensor_tensor(
+                pulled[:],
+                h[t][:].indirect(offsets[d][:, v0 // 16 : (v0 + width) // 16]),
+                neg_gate[d][:, v0 : v0 + width],
+                MULT,
+            )
+            turn_into(sums, pulled, width, False, d == 1)
+            if d == 1:
+                nc.scalar.copy(
+                    out=z_rows[chunk][:, :, :, 32 * t : 32 * (t + 1), :],
+                    in_=sums[:, 0:width].rearrange("v (b q u e) -> v b u q e", b=width // P, u=2, e=2),
+                )
+                if t == TILES - 1:
+                    grouped_z.append(finish_chunk(chunk, z_rows[chunk]))
+        for chunk in (2, 0, 1):
+            project_chunk(chunk, grouped_z[chunk])

@@ -21,10 +21,24 @@ P = 128
 PACK = 4
 BANK = 512
 TILES = H // P
+LISTS = 2
+QUADRANT = 32
+LIST_ROWS = 16
+
 CHUNKS = ((0, 512), (512, 384), (896, 128))
+LAST = len(CHUNKS) - 1
+PIECES = {512: (512,), 384: (256, 128), 128: (128,)}
 SLOTS = 6
-AHEAD = 1
-PIECES = {512: (512,), 384: (256, 128), 256: (256,), 128: (128,)}
+LAST_SLOTS = 3
+W1_SLOT = 4
+AHEAD = 2
+
+GATE_BANKS = (0, 1)
+H_BANKS = ((0, 1), (2, 3), (0, 1), (2, 3))
+SUM_BANKS = (4, 5, 6, 7)
+LAST_SUM_BANKS = (2, 3)
+PAIR_BANKS = (0, 1)
+OUT_BANKS = ((4,), (5, 6), (7,))
 
 
 def tile_picked_wlapl_none_l_kernel(
@@ -40,102 +54,97 @@ def tile_picked_wlapl_none_l_kernel(
         def bank(index, name):
             return psum.tile([P, BANK], F32, name=name, tag="bank%d" % index)
 
+        def slot_tag(n):
+            return "slot%d" % (n % SLOTS)
+
         x_plane = keep.tile([P, T], U8, name="x_plane", align_bytes=64)
         w2_plane = keep.tile([P, N], U8, name="w2_plane", align_bytes=64)
         ident = keep.tile([P, P], F32, name="ident")
         make_identity(nc, ident[:])
 
         w1_rows = w1.rearrange("(p j) c -> p j c", j=PACK)
-        w1_loads = ((0, 1), (1, 3))
-        w1_raw = [keep.tile([P, PACK, n * P], F32, name="w1_raw%d" % t) for t, n in w1_loads]
+        w1_first = keep.tile([P, PACK, P], F32, name="w1_first")
+        w1_rest = keep.tile([P, PACK, H - P], F32, name="w1_rest")
         x_codes = keep.tile([P, T], U32, name="x_codes", align_bytes=64)
-        gate_cols = keep.tile([P, 2, T // P], F32, name="gate_cols")
-        offsets = [lists.tile([P, T // 16], U16, name="offsets%d" % d) for d in range(2)]
+        gate_cols = keep.tile([P, LISTS, T // P], F32, name="gate_cols")
+        offsets = [lists.tile([P, T // LIST_ROWS], U16, name="offsets%d" % d) for d in range(LISTS)]
         w2_codes = keep.tile([P, 2 * N], U8, name="w2_codes", align_bytes=64)
 
+        def load_scales(queue, plane, scales):
+            for q in range(P // QUADRANT):
+                queue.dma_start(
+                    out=plane[QUADRANT * q : QUADRANT * (q + 1), :].bitcast(I32),
+                    in_=scales[0, 4 * q : 4 * q + 4, :].bitcast(I32).partition_broadcast(QUADRANT // 4),
+                )
+
         nc.sync.dma_start(out=gate_cols[:], in_=gate[:, 0, :].rearrange("d (p j) -> p d j", p=P))
-        nc.sync.dma_start(out=w1_raw[0][:], in_=w1_rows[:, :, 0:P])
-        for q in range(4):
-            nc.scalar.dma_start(
-                out=x_plane[32 * q : 32 * (q + 1), :].bitcast(I32),
-                in_=x_scales[0, 4 * q : 4 * q + 4, :].bitcast(I32).partition_broadcast(8),
-            )
+        nc.sync.dma_start(out=w1_first[:], in_=w1_rows[:, :, 0:P])
+        load_scales(nc.scalar, x_plane, x_scales)
         nc.sync.dma_start(out=x_codes[:].bitcast(I32), in_=x_words[0].rearrange("p c r -> p (c r)").bitcast(I32))
         nc.sync.dma_start(offsets[0][:], pos1)
-        nc.sync.dma_start(out=w1_raw[1][:], in_=w1_rows[:, :, P : 4 * P])
+        nc.sync.dma_start(out=w1_rest[:], in_=w1_rows[:, :, P:H])
         nc.sync.dma_start(offsets[1][:], pos2)
         nc.sync.dma_start(out=w2_codes[:].bitcast(I32), in_=w2_words[0].bitcast(I32))
-        for q in range(4):
-            nc.sync.dma_start(
-                out=w2_plane[32 * q : 32 * (q + 1), :].bitcast(I32),
-                in_=w2_scales[0, 4 * q : 4 * q + 4, :].bitcast(I32).partition_broadcast(8),
-            )
+        load_scales(nc.sync, w2_plane, w2_scales)
 
-        neg_gate = [keep.tile([P, T], F32, name="neg_gate%d" % d) for d in range(2)]
+        neg_gate = [keep.tile([P, T], F32, name="neg_gate%d" % d) for d in range(LISTS)]
 
-        def slot_of(n):
-            return "slot%d" % (n % 4 if n < 6 else (n - 2) % SLOTS)
-
-        def spread_gate(d, b, index):
-            spread = bank(index, "spread")
-            for j in range(PACK):
-                nc.tensor.transpose(
-                    spread[:, j * P : (j + 1) * P], gate_cols[:, d, PACK * b + j : PACK * b + j + 1].to_broadcast([P, P]), ident[:]
+        def spread_gate(d):
+            for half, index in enumerate(GATE_BANKS):
+                spread = bank(index, "spread")
+                for j in range(PACK):
+                    column = PACK * half + j
+                    nc.tensor.transpose(
+                        spread[:, j * P : (j + 1) * P],
+                        gate_cols[:, d, column : column + 1].to_broadcast([P, P]),
+                        ident[:],
+                    )
+                nc.scalar.activation(
+                    out=neg_gate[d][:].rearrange("p (i b j) -> p b i j", b=2, j=PACK)[:, half],
+                    in_=spread[:].rearrange("p (j i) -> p i j", j=PACK),
+                    func=COPY,
+                    scale=-1.0,
                 )
-            nc.scalar.activation(
-                out=neg_gate[d][:].rearrange("p (i b j) -> p b i j", b=2, j=PACK)[:, b],
-                in_=spread[:].rearrange("p (j i) -> p i j", j=PACK),
-                func=COPY,
-                scale=-1.0,
-            )
 
-        grouped_tags = ("slot0", "w1_codes0", "slot0", "slot1")
-        w1_codes = [
-            ring.tile([P, P], U32, name="w1_codes", tag="w1_codes%d" % t, align_bytes=64) for t in range(TILES)
-        ]
-        w1_plane = [keep.tile([P, P], U8, name="w1_plane%d" % t, align_bytes=64) for t in range(TILES)]
         h = [keep.tile([P, T], F32, name="h%d" % t) for t in range(TILES)]
+        w1_codes, w1_plane = {}, {}
 
-        def quantize_w1(t):
-            grouped = ring.tile([P, P, PACK], BF16, name="w1_grouped", tag=grouped_tags[t], align_bytes=64)
-            dst = grouped[:].rearrange("p (c i) j -> p c j i", i=4)
-            first = t - min(t, 1)
-            src = w1_raw[min(t, 1)][:, :, first * P : (first + 1) * P].rearrange("p j (c i) -> p c j i", i=4)
-            if t < 1:
-                nc.vector.tensor_copy(out=dst, in_=src)
-            else:
-                nc.scalar.copy(out=dst, in_=src)
-            nc.vector.quantize_mx(
-                out=w1_codes[t][:].bitcast(FP8X4),
-                scales=w1_plane[t][:],
-                in_=grouped[:].rearrange("p c j -> p (c j)"),
+        def quantize_w1(tiles, raw, cast, codes_tag, grouped_tag):
+            width = len(tiles) * P
+            codes = ring.tile([P, width], U32, name="w1_codes", tag=codes_tag, align_bytes=64)
+            plane = keep.tile([P, width], U8, name="w1_plane%d" % tiles[0], align_bytes=64)
+            grouped = ring.tile([P, width, PACK], BF16, name="w1_grouped", tag=grouped_tag, align_bytes=64)
+            cast(
+                out=grouped[:].rearrange("p (c i) j -> p c j i", i=4),
+                in_=raw.rearrange("p j (c i) -> p c j i", i=4),
             )
+            nc.vector.quantize_mx(
+                out=codes[:].bitcast(FP8X4), scales=plane[:], in_=grouped[:].rearrange("p c j -> p (c j)")
+            )
+            for n, t in enumerate(tiles):
+                w1_codes[t] = codes[:, n * P : (n + 1) * P]
+                w1_plane[t] = plane[:, n * P : (n + 1) * P]
 
-        h_banks = (0, 2, 0, 2)
-
-        def project(t):
-            for half in range(2):
+        def project(t, evacuate):
+            for half, index in enumerate(H_BANKS[t]):
                 cols = slice(half * BANK, (half + 1) * BANK)
-                acc = bank(h_banks[t] + half, "h_acc")
+                acc = bank(index, "h_acc")
                 nc.tensor.matmul_mx(
                     out=acc[:],
-                    lhsT=w1_codes[t][:].bitcast(FP8X4),
-                    lhsT_scale=w1_plane[t][:],
+                    lhsT=w1_codes[t].bitcast(FP8X4),
+                    lhsT_scale=w1_plane[t],
                     rhs=x_codes[:, cols].bitcast(FP8X4),
                     rhs_scale=x_plane[:, cols],
                     start=True,
                     stop=True,
                 )
-                if t == 0:
-                    nc.vector.tensor_copy(out=h[t][:, cols], in_=acc[:])
-                else:
-                    nc.scalar.copy(out=h[t][:, cols], in_=acc[:])
+                evacuate(out=h[t][:, cols], in_=acc[:])
 
-        def turn_into(sums, term, width, first, last):
-            blocks = width // P
+        def turn_into(region, term, first, last):
+            blocks = term.shape[1] // P
             for b in range(blocks):
                 nc.tensor.matmul(
-                    sums[:, b * P : (b + 1) * P],
+                    region[:, b * P : (b + 1) * P],
                     term[:, b * P : (b + 1) * P],
                     ident[:],
                     start=(first and b == 0),
@@ -143,52 +152,69 @@ def tile_picked_wlapl_none_l_kernel(
                     is_transpose=True,
                 )
 
-        steps = [(0, 0), (1, 0)] + [
-            (chunk, t) for chunk in range(len(CHUNKS)) for t in range(TILES) if t > 0 or chunk > 1
+        early = [(0, 0), (1, 0)] + [(chunk, t) for chunk in range(LAST) for t in range(1, TILES)]
+        sums = [(chunk, (t,), SUM_BANKS[s % len(SUM_BANKS)]) for s, (chunk, t) in enumerate(early)]
+        sums.append((LAST, tuple(range(TILES - 1)), LAST_SUM_BANKS[0]))
+        sums.append((LAST, (TILES - 1,), LAST_SUM_BANKS[1]))
+        opened = {}
+
+        def open_sum(s):
+            chunk, tiles, index = sums[s]
+            v0, width = CHUNKS[chunk]
+            opened[s] = bank(index, "sum")
+            for n, t in enumerate(tiles):
+                turn_into(opened[s][:, n * width : (n + 1) * width], h[t][:, v0 : v0 + width], n == 0, False)
+
+        z_rows = [
+            keep.tile([P, width // P, 2, P, 2], BF16, name="z_rows%d" % chunk)
+            for chunk, (v0, width) in enumerate(CHUNKS)
         ]
-        open_sums = {}
 
-        def open_step(s):
-            chunk, t = steps[s]
-            v0, width = CHUNKS[chunk]
-            open_sums[s] = bank(4 + s % 4, "sums")
-            turn_into(open_sums[s], h[t][:, v0 : v0 + width], width, True, False)
+        def close_sum(s):
+            chunk, tiles, index = sums[s]
+            width = CHUNKS[chunk][1]
+            words_per_tile = P // PACK
+            nc.scalar.copy(
+                out=z_rows[chunk][:, :, :, words_per_tile * tiles[0] : words_per_tile * (tiles[-1] + 1), :],
+                in_=opened[s][:, 0 : len(tiles) * width].rearrange(
+                    "v (b p u e) -> v b u p e", b=width // P, u=2, e=2
+                ),
+            )
 
-        def finish_chunk(chunk, z_rows):
-            v0, width = CHUNKS[chunk]
+        def turn_back(chunk):
+            width = CHUNKS[chunk][1]
             blocks = width // P
-            z_words = z_rows[:].rearrange("v b u p e -> v (b u p e)").bitcast(F32)
+            pairs = z_rows[chunk][:].rearrange("v b u p e -> v (b u p e)").bitcast(F32)
             z_grouped = keep.tile([P, width * PACK], BF16, name="z_grouped%d" % chunk, align_bytes=64)
             for b0 in range(0, blocks, 2):
                 count = min(2, blocks - b0)
-                words = bank((b0 // 2 + chunk) % 2, "words")
-                for s in range(2 * count):
+                turned = bank(PAIR_BANKS[(b0 // 2 + chunk) % 2], "turned")
+                for n in range(2 * count):
                     nc.tensor.transpose(
-                        words[:, s * P : (s + 1) * P],
-                        z_words[:, (2 * b0 + s) * P : (2 * b0 + s + 1) * P],
+                        turned[:, n * P : (n + 1) * P],
+                        pairs[:, (2 * b0 + n) * P : (2 * b0 + n + 1) * P],
                         ident[:],
                     )
                 nc.scalar.copy(
                     out=z_grouped[:, b0 * P * PACK : (b0 + count) * P * PACK]
                     .bitcast(F32)
                     .rearrange("p (b v u) -> p b v u", b=count, u=2),
-                    in_=words[:, 0 : 2 * count * P].rearrange("p (b u v) -> p b v u", b=count, u=2),
+                    in_=turned[:, 0 : 2 * count * P].rearrange("p (b u v) -> p b v u", b=count, u=2),
                 )
             return z_grouped
 
-        def project_chunk(chunk, z_grouped):
+        def project_chunk(chunk, z_grouped, codes_tags, evacuate):
             v0, width = CHUNKS[chunk]
             c0 = 0
             for n, piece in enumerate(PIECES[width]):
-                tag = slot_of(len(pulls) - 2) if chunk == 0 else "z_codes%d_%d" % (chunk, n)
-                z_codes = ring.tile([P, piece], U32, name="z_codes", tag=tag, align_bytes=64)
+                z_codes = ring.tile([P, piece], U32, name="z_codes", tag=codes_tags[n], align_bytes=64)
                 z_plane = keep.tile([P, piece], U8, name="z_plane%d_%d" % (chunk, n), align_bytes=64)
                 nc.vector.quantize_mx(
                     out=z_codes[:].bitcast(FP8X4),
                     scales=z_plane[:],
                     in_=z_grouped[:, c0 * PACK : (c0 + piece) * PACK],
                 )
-                acc = bank((2, 4, 3)[chunk] + n, "out_acc")
+                acc = bank(OUT_BANKS[chunk][n], "out_acc")
                 nc.tensor.matmul_mx(
                     out=acc[:, 0:piece],
                     lhsT=w2_codes[:].bitcast(FP4X4),
@@ -199,52 +225,51 @@ def tile_picked_wlapl_none_l_kernel(
                     stop=True,
                 )
                 result = keep.tile([P, piece], F32, name="result%d_%d" % (chunk, n))
-                if chunk == 0:
-                    nc.vector.tensor_copy(out=result[:], in_=acc[:, 0:piece])
-                else:
-                    nc.scalar.copy(out=result[:], in_=acc[:, 0:piece])
+                evacuate(out=result[:], in_=acc[:, 0:piece])
                 nc.sync.dma_start(out=out[:, v0 + c0 : v0 + c0 + piece], in_=result[:])
                 c0 += piece
 
-        spread_gate(0, 0, 0)
-        spread_gate(0, 1, 1)
-        quantize_w1(0)
-        project(0)
-        spread_gate(1, 0, 0)
-        spread_gate(1, 1, 1)
-        quantize_w1(1)
-        project(1)
+        spread_gate(0)
+        quantize_w1((0,), w1_first[:], nc.vector.tensor_copy, slot_tag(W1_SLOT), slot_tag(0))
+        project(0, nc.vector.tensor_copy)
+        spread_gate(1)
+        quantize_w1((1,), w1_rest[:, :, 0:P], nc.scalar.copy, "w1_codes1", slot_tag(W1_SLOT))
+        project(1, nc.scalar.copy)
 
-        z_rows = [
-            keep.tile([P, width // P, 2, P, 2], BF16, name="z_rows%d" % chunk)
-            for chunk, (v0, width) in enumerate(CHUNKS)
-        ]
-        grouped_z = []
-        pulls = [(0, 0), (1, 0), (0, 1), (1, 1)] + [(s, d) for s in range(2, len(steps)) for d in range(2)]
-        for n, (s, d) in enumerate(pulls):
-            chunk, t = steps[s]
+        pulls = [(s, 0, d) for d in range(LISTS) for s in range(2)]
+        pulls.extend((s, n, d) for s in range(2, len(sums)) for n in range(len(sums[s][1])) for d in range(LISTS))
+        wide_pulls = LISTS * len(early)
+        tags = [slot_tag(count) for count in range(wide_pulls)]
+        for count in range(wide_pulls, len(pulls)):
+            tags.append(tags[count - LAST_SLOTS])
+        z_grouped = []
+        for count, (s, n, d) in enumerate(pulls):
+            chunk, tiles, index = sums[s]
             v0, width = CHUNKS[chunk]
-            if n in (1, 2):
-                quantize_w1(n + 1)
-                project(n + 1)
-            for ahead in range(s, min(s + AHEAD + 1, len(steps))):
-                if ahead not in open_sums:
-                    open_step(ahead)
-            sums = open_sums[s]
-            pulled = ring.tile([P, width], F32, name="pulled", tag=slot_of(n), align_bytes=64)
+            if count == 1:
+                quantize_w1((2, 3), w1_rest[:, :, P : 3 * P], nc.scalar.copy, "w1_codes2", slot_tag(W1_SLOT))
+                project(2, nc.scalar.copy)
+                project(3, nc.scalar.copy)
+            wanted = list(range(s, min(s + AHEAD + 1, len(early))))
+            if (chunk, tiles) == (0, (TILES - 1,)):
+                wanted.extend(range(len(early), len(sums)))
+            for ahead in wanted:
+                if ahead not in opened:
+                    open_sum(ahead)
+            pulled = ring.tile([P, width], F32, name="pulled", tag=tags[count], align_bytes=64)
             nc.vector.tensor_tensor(
                 pulled[:],
-                h[t][:].indirect(offsets[d][:, v0 // 16 : (v0 + width) // 16]),
+                h[tiles[n]][:].indirect(offsets[d][:, v0 // LIST_ROWS : (v0 + width) // LIST_ROWS]),
                 neg_gate[d][:, v0 : v0 + width],
                 MULT,
             )
-            turn_into(sums, pulled, width, False, d == 1)
-            if d == 1:
-                nc.scalar.copy(
-                    out=z_rows[chunk][:, :, :, 32 * t : 32 * (t + 1), :],
-                    in_=sums[:, 0:width].rearrange("v (b q u e) -> v b u q e", b=width // P, u=2, e=2),
-                )
-                if t == TILES - 1:
-                    grouped_z.append(finish_chunk(chunk, z_rows[chunk]))
-        for chunk in (2, 0, 1):
-            project_chunk(chunk, grouped_z[chunk])
+            complete = n == len(tiles) - 1 and d == LISTS - 1
+            turn_into(opened[s][:, n * width : (n + 1) * width], pulled[:], False, complete)
+            if complete:
+                close_sum(s)
+                if tiles[-1] == TILES - 1:
+                    z_grouped.append(turn_back(chunk))
+
+        project_chunk(LAST, z_grouped[LAST], ("z_codes2",), nc.scalar.copy)
+        project_chunk(0, z_grouped[0], (tags[-2],), nc.vector.tensor_copy)
+        project_chunk(1, z_grouped[1], ("z_codes1a", "z_codes1b"), nc.scalar.copy)

from contextlib import ExitStack

import concourse.mybir as mybir
from concourse.masks import make_identity

K, T, H, N = 512, 1024, 512, 128
FLOPS = 2 * K * H * T + 2 * H * N * T

F32 = mybir.dt.float32
BF16 = mybir.dt.bfloat16
I32 = mybir.dt.int32
U32 = mybir.dt.uint32
U16 = mybir.dt.uint16
U8 = mybir.dt.uint8
FP8X4 = mybir.dt.float8_e4m3fn_x4
FP4X4 = mybir.dt.float4_e2m1fn_x4
MULT = mybir.AluOpType.mult
COPY = mybir.ActivationFunctionType.Copy

P = 128
PACK = 4
BANK = 512
TILES = H // P
LISTS = 2
QUADRANT = 32
LIST_ROWS = 16

CHUNKS = ((0, 512), (512, 384), (896, 128))
LAST = len(CHUNKS) - 1
PIECES = {512: (512,), 384: (256, 128), 128: (128,)}
SLOTS = 6
LAST_SLOTS = 3
W1_SLOT = 4
AHEAD = 2

GATE_BANKS = (0, 1)
H_BANKS = ((0, 1), (2, 3), (0, 1), (2, 3))
SUM_BANKS = (4, 5, 6, 7)
LAST_SUM_BANKS = (2, 3)
PAIR_BANKS = (0, 1)
OUT_BANKS = ((4,), (5, 6), (7,))


def tile_picked_wlapl_none_l_kernel(
    tc, x_words, x_scales, w1, w2_words, w2_scales, gate, pos1, pos2, out
):
    nc = tc.nc
    with ExitStack() as ctx:
        lists = ctx.enter_context(tc.tile_pool(name="lists", bufs=1))
        keep = ctx.enter_context(tc.tile_pool(name="keep", bufs=1))
        ring = ctx.enter_context(tc.tile_pool(name="ring", bufs=1))
        psum = ctx.enter_context(tc.psum_pool(name="psum", bufs=1))

        def bank(index, name):
            return psum.tile([P, BANK], F32, name=name, tag="bank%d" % index)

        def slot_tag(n):
            return "slot%d" % (n % SLOTS)

        x_plane = keep.tile([P, T], U8, name="x_plane", align_bytes=64)
        w2_plane = keep.tile([P, N], U8, name="w2_plane", align_bytes=64)
        ident = keep.tile([P, P], F32, name="ident")
        make_identity(nc, ident[:])

        w1_rows = w1.rearrange("(p j) c -> p j c", j=PACK)
        w1_first = keep.tile([P, PACK, P], F32, name="w1_first")
        w1_rest = keep.tile([P, PACK, H - P], F32, name="w1_rest")
        x_codes = keep.tile([P, T], U32, name="x_codes", align_bytes=64)
        gate_cols = keep.tile([P, LISTS, T // P], F32, name="gate_cols")
        offsets = [lists.tile([P, T // LIST_ROWS], U16, name="offsets%d" % d) for d in range(LISTS)]
        w2_codes = keep.tile([P, 2 * N], U8, name="w2_codes", align_bytes=64)

        def load_scales(queue, plane, scales):
            for q in range(P // QUADRANT):
                queue.dma_start(
                    out=plane[QUADRANT * q : QUADRANT * (q + 1), :].bitcast(I32),
                    in_=scales[0, 4 * q : 4 * q + 4, :].bitcast(I32).partition_broadcast(QUADRANT // 4),
                )

        nc.sync.dma_start(out=gate_cols[:], in_=gate[:, 0, :].rearrange("d (p j) -> p d j", p=P))
        nc.sync.dma_start(out=w1_first[:], in_=w1_rows[:, :, 0:P])
        load_scales(nc.scalar, x_plane, x_scales)
        nc.sync.dma_start(out=x_codes[:].bitcast(I32), in_=x_words[0].rearrange("p c r -> p (c r)").bitcast(I32))
        nc.sync.dma_start(offsets[0][:], pos1)
        nc.sync.dma_start(out=w1_rest[:], in_=w1_rows[:, :, P:H])
        nc.sync.dma_start(offsets[1][:], pos2)
        nc.sync.dma_start(out=w2_codes[:].bitcast(I32), in_=w2_words[0].bitcast(I32))
        load_scales(nc.sync, w2_plane, w2_scales)

        neg_gate = [keep.tile([P, T], F32, name="neg_gate%d" % d) for d in range(LISTS)]

        def spread_gate(d):
            for half, index in enumerate(GATE_BANKS):
                spread = bank(index, "spread")
                for j in range(PACK):
                    column = PACK * half + j
                    nc.tensor.transpose(
                        spread[:, j * P : (j + 1) * P],
                        gate_cols[:, d, column : column + 1].to_broadcast([P, P]),
                        ident[:],
                    )
                nc.scalar.activation(
                    out=neg_gate[d][:].rearrange("p (i b j) -> p b i j", b=2, j=PACK)[:, half],
                    in_=spread[:].rearrange("p (j i) -> p i j", j=PACK),
                    func=COPY,
                    scale=-1.0,
                )

        h = [keep.tile([P, T], F32, name="h%d" % t) for t in range(TILES)]
        w1_codes, w1_plane = {}, {}

        def quantize_w1(tiles, raw, cast, codes_tag, grouped_tag):
            width = len(tiles) * P
            codes = ring.tile([P, width], U32, name="w1_codes", tag=codes_tag, align_bytes=64)
            plane = keep.tile([P, width], U8, name="w1_plane%d" % tiles[0], align_bytes=64)
            grouped = ring.tile([P, width, PACK], BF16, name="w1_grouped", tag=grouped_tag, align_bytes=64)
            cast(
                out=grouped[:].rearrange("p (c i) j -> p c j i", i=4),
                in_=raw.rearrange("p j (c i) -> p c j i", i=4),
            )
            nc.vector.quantize_mx(
                out=codes[:].bitcast(FP8X4), scales=plane[:], in_=grouped[:].rearrange("p c j -> p (c j)")
            )
            for n, t in enumerate(tiles):
                w1_codes[t] = codes[:, n * P : (n + 1) * P]
                w1_plane[t] = plane[:, n * P : (n + 1) * P]

        def project(t, evacuate):
            for half, index in enumerate(H_BANKS[t]):
                cols = slice(half * BANK, (half + 1) * BANK)
                acc = bank(index, "h_acc")
                nc.tensor.matmul_mx(
                    out=acc[:],
                    lhsT=w1_codes[t].bitcast(FP8X4),
                    lhsT_scale=w1_plane[t],
                    rhs=x_codes[:, cols].bitcast(FP8X4),
                    rhs_scale=x_plane[:, cols],
                    start=True,
                    stop=True,
                )
                evacuate(out=h[t][:, cols], in_=acc[:])

        def turn_into(region, term, first, last):
            blocks = term.shape[1] // P
            for b in range(blocks):
                nc.tensor.matmul(
                    region[:, b * P : (b + 1) * P],
                    term[:, b * P : (b + 1) * P],
                    ident[:],
                    start=(first and b == 0),
                    stop=(last and b == blocks - 1),
                    is_transpose=True,
                )

        early = [(0, 0), (1, 0)] + [(chunk, t) for chunk in range(LAST) for t in range(1, TILES)]
        sums = [(chunk, (t,), SUM_BANKS[s % len(SUM_BANKS)]) for s, (chunk, t) in enumerate(early)]
        sums.append((LAST, tuple(range(TILES - 1)), LAST_SUM_BANKS[0]))
        sums.append((LAST, (TILES - 1,), LAST_SUM_BANKS[1]))
        opened = {}

        def open_sum(s):
            chunk, tiles, index = sums[s]
            v0, width = CHUNKS[chunk]
            opened[s] = bank(index, "sum")
            for n, t in enumerate(tiles):
                turn_into(opened[s][:, n * width : (n + 1) * width], h[t][:, v0 : v0 + width], n == 0, False)

        z_rows = [
            keep.tile([P, width // P, 2, P, 2], BF16, name="z_rows%d" % chunk)
            for chunk, (v0, width) in enumerate(CHUNKS)
        ]

        def close_sum(s):
            chunk, tiles, index = sums[s]
            width = CHUNKS[chunk][1]
            words_per_tile = P // PACK
            nc.scalar.copy(
                out=z_rows[chunk][:, :, :, words_per_tile * tiles[0] : words_per_tile * (tiles[-1] + 1), :],
                in_=opened[s][:, 0 : len(tiles) * width].rearrange(
                    "v (b p u e) -> v b u p e", b=width // P, u=2, e=2
                ),
            )

        def turn_back(chunk):
            width = CHUNKS[chunk][1]
            blocks = width // P
            pairs = z_rows[chunk][:].rearrange("v b u p e -> v (b u p e)").bitcast(F32)
            z_grouped = keep.tile([P, width * PACK], BF16, name="z_grouped%d" % chunk, align_bytes=64)
            for b0 in range(0, blocks, 2):
                count = min(2, blocks - b0)
                turned = bank(PAIR_BANKS[(b0 // 2 + chunk) % 2], "turned")
                for n in range(2 * count):
                    nc.tensor.transpose(
                        turned[:, n * P : (n + 1) * P],
                        pairs[:, (2 * b0 + n) * P : (2 * b0 + n + 1) * P],
                        ident[:],
                    )
                nc.scalar.copy(
                    out=z_grouped[:, b0 * P * PACK : (b0 + count) * P * PACK]
                    .bitcast(F32)
                    .rearrange("p (b v u) -> p b v u", b=count, u=2),
                    in_=turned[:, 0 : 2 * count * P].rearrange("p (b u v) -> p b v u", b=count, u=2),
                )
            return z_grouped

        def project_chunk(chunk, z_grouped, codes_tags, evacuate):
            v0, width = CHUNKS[chunk]
            c0 = 0
            for n, piece in enumerate(PIECES[width]):
                z_codes = ring.tile([P, piece], U32, name="z_codes", tag=codes_tags[n], align_bytes=64)
                z_plane = keep.tile([P, piece], U8, name="z_plane%d_%d" % (chunk, n), align_bytes=64)
                nc.vector.quantize_mx(
                    out=z_codes[:].bitcast(FP8X4),
                    scales=z_plane[:],
                    in_=z_grouped[:, c0 * PACK : (c0 + piece) * PACK],
                )
                acc = bank(OUT_BANKS[chunk][n], "out_acc")
                nc.tensor.matmul_mx(
                    out=acc[:, 0:piece],
                    lhsT=w2_codes[:].bitcast(FP4X4),
                    lhsT_scale=w2_plane[:],
                    rhs=z_codes[:].bitcast(FP8X4),
                    rhs_scale=z_plane[:],
                    start=True,
                    stop=True,
                )
                result = keep.tile([P, piece], F32, name="result%d_%d" % (chunk, n))
                evacuate(out=result[:], in_=acc[:, 0:piece])
                nc.sync.dma_start(out=out[:, v0 + c0 : v0 + c0 + piece], in_=result[:])
                c0 += piece

        spread_gate(0)
        quantize_w1((0,), w1_first[:], nc.vector.tensor_copy, slot_tag(W1_SLOT), slot_tag(0))
        project(0, nc.vector.tensor_copy)
        spread_gate(1)
        quantize_w1((1,), w1_rest[:, :, 0:P], nc.scalar.copy, "w1_codes1", slot_tag(W1_SLOT))
        project(1, nc.scalar.copy)

        pulls = [(s, 0, d) for d in range(LISTS) for s in range(2)]
        pulls.extend((s, n, d) for s in range(2, len(sums)) for n in range(len(sums[s][1])) for d in range(LISTS))
        wide_pulls = LISTS * len(early)
        tags = [slot_tag(count) for count in range(wide_pulls)]
        for count in range(wide_pulls, len(pulls)):
            tags.append(tags[count - LAST_SLOTS])
        z_grouped = []
        for count, (s, n, d) in enumerate(pulls):
            chunk, tiles, index = sums[s]
            v0, width = CHUNKS[chunk]
            if count == 1:
                quantize_w1((2, 3), w1_rest[:, :, P : 3 * P], nc.scalar.copy, "w1_codes2", slot_tag(W1_SLOT))
                project(2, nc.scalar.copy)
                project(3, nc.scalar.copy)
            wanted = list(range(s, min(s + AHEAD + 1, len(early))))
            if (chunk, tiles) == (0, (TILES - 1,)):
                wanted.extend(range(len(early), len(sums)))
            for ahead in wanted:
                if ahead not in opened:
                    open_sum(ahead)
            pulled = ring.tile([P, width], F32, name="pulled", tag=tags[count], align_bytes=64)
            nc.vector.tensor_tensor(
                pulled[:],
                h[tiles[n]][:].indirect(offsets[d][:, v0 // LIST_ROWS : (v0 + width) // LIST_ROWS]),
                neg_gate[d][:, v0 : v0 + width],
                MULT,
            )
            complete = n == len(tiles) - 1 and d == LISTS - 1
            turn_into(opened[s][:, n * width : (n + 1) * width], pulled[:], False, complete)
            if complete:
                close_sum(s)
                if tiles[-1] == TILES - 1:
                    z_grouped.append(turn_back(chunk))

        project_chunk(LAST, z_grouped[LAST], ("z_codes2",), nc.scalar.copy)
        project_chunk(0, z_grouped[0], (tags[-2],), nc.vector.tensor_copy)
        project_chunk(1, z_grouped[1], ("z_codes1a", "z_codes1b"), nc.scalar.copy)
